import numpy as np
import ml_dtypes


def mxq(x, axis, fmt="e4m3"):
    dtype, down = {"e4m3": (ml_dtypes.float8_e4m3fn, 7), "e5m2": (ml_dtypes.float8_e5m2, 14)}[fmt]
    v = np.moveaxis(np.asarray(x, np.float32).astype(ml_dtypes.bfloat16).astype(np.float64), axis, -1)
    blocks = v.reshape(v.shape[:-1] + (-1, 32))
    amax = np.abs(blocks).max(-1, keepdims=True)
    byte = np.maximum(np.where(amax > 0, np.frexp(amax)[1] - 1 + 127, 0) - down, 1)
    scale = np.exp2(byte - 127.0)
    codes = (blocks / scale).astype(np.float32).astype(dtype).astype(np.float64)
    return np.moveaxis((codes * scale).reshape(v.shape), -1, axis)


WIDE = False


def mx_kscale(k):
    if not WIDE:
        return np.ones(k)
    levels = np.array([30, -30])
    if k % 512:
        return np.exp2(np.random.permutation(np.resize(levels, k // 32))).repeat(32)
    a = np.empty((k // 512, 16))
    for p in range(k // 512):
        a[p, :8] = np.random.permutation(np.resize(levels, 8))
        for g in range(8):
            far = levels[np.abs(levels - a[p, g]) >= 10]
            a[p, g + 8] = far[np.random.randint(len(far))]
    return np.exp2(a.ravel()).repeat(32)


def f64(x):
    return np.asarray(x).astype(np.float64)


def striped(idx):
    return np.tile(np.asarray(idx).reshape(-1, 16).T, (8, 1)).astype(np.uint16)


def unstriped(offs):
    return offs[:16].T.reshape(-1).astype(np.int64)


E2M1 = np.array([0.0, 0.5, 1.0, 1.5, 2.0, 3.0, 4.0, 6.0, -0.0, -0.5, -1.0, -1.5, -2.0, -3.0, -4.0, -6.0])


def pack_weight(w, fmt):
    k, n = w.shape
    w = f64(np.asarray(w, np.float32).astype(ml_dtypes.bfloat16)).reshape(k // 32, 32, n)
    amax = np.abs(w).max(1)
    if fmt in ("e4m3", "e5m2"):
        byte = np.frexp(amax)[1] - 1 + 127 - (7 if fmt == "e4m3" else 14)
    else:
        mant, ex = np.frexp(amax / 6.0)
        byte = np.where(mant > 0.5, ex, ex - 1) + 127
    byte = np.clip(np.where(amax > 0, byte, 1), 1, 254)
    scaled = (w * np.exp2(127.0 - byte)[:, None, :]).reshape(k, n).astype(np.float32)
    by_word = np.ascontiguousarray(scaled.reshape(k // 512, 128, 4, n).transpose(0, 1, 3, 2))
    if fmt in ("e4m3", "e5m2"):
        words = by_word.astype(ml_dtypes.float8_e4m3fn if fmt == "e4m3" else ml_dtypes.float8_e5m2).view(np.uint8)
    else:
        c = by_word.astype(ml_dtypes.float4_e2m1fn).view(np.uint8) & 0xF
        words = (c[..., 0::2] | (c[..., 1::2] << 4)).reshape(k // 512, 128, 2 * n)
    return np.ascontiguousarray(words), np.ascontiguousarray(byte.astype(np.uint8).reshape(k // 512, 16, n))


def unpack_weight(words, scales, fmt):
    g, _, n = scales.shape
    words = np.ascontiguousarray(words).reshape(g, 128, n, -1)
    if fmt in ("e4m3", "e5m2"):
        vals = words.view(ml_dtypes.float8_e4m3fn if fmt == "e4m3" else ml_dtypes.float8_e5m2).astype(np.float64)
    else:
        nib = np.empty((g, 128, n, 4), np.uint8)
        nib[..., 0::2] = words & 0xF
        nib[..., 1::2] = words >> 4
        vals = E2M1[nib]
    vals = vals * np.repeat(np.exp2(scales.astype(np.float64) - 127.0), 8, axis=1)[..., None]
    return vals.transpose(0, 1, 3, 2).reshape(g * 512, n)


def e4m3fn_bytes(y):
    return np.clip(np.asarray(y, np.float64), -448.0, 448.0).astype(np.float32).astype(ml_dtypes.float8_e4m3fn).view(np.uint8)


def e4m3fn_values(b):
    return np.asarray(b, np.uint8).view(ml_dtypes.float8_e4m3fn).astype(np.float64)


K, T, J, R, V, D, I, N, E = 512, 1024, 256, 512, 1024, 2048, 1024, 256, 512


def setup_inputs():
    n = np.random.standard_normal
    idx = np.random.permutation(V)[:R]
    idx2 = np.random.permutation(T)[:J]
    idx3 = np.random.permutation(D)[:I]
    idx4 = np.random.permutation(E)[:J]
    fk = mx_kscale(K)
    fr = mx_kscale(R)
    xtp = pack_weight(n((K, T)) / fk[:, None], "e4m3")
    wtp = pack_weight(n((K, V)) * 1 / np.sqrt(K) * fk[:, None], "e2m1")
    wbp = pack_weight(n((R, N)) * 1 / np.sqrt(R) / fr[:, None], "e5m2")
    return {
        "xt_words": xtp[0],
        "xt_scales": xtp[1],
        "wt_words": wtp[0],
        "wt_scales": wtp[1],
        "ca": e4m3fn_bytes(60.0 * n((R, D))),
        "st": (np.random.uniform(0.004, 0.012, (R, 1)) * fr[:, None]).astype(np.float32),
        "wb_words": wbp[0],
        "wb_scales": wbp[1],
        "so": (np.random.uniform(0.5, 1.6, (N, 1))).astype(np.float32),
        "offs": striped(idx),
        "offs2": striped(idx2),
        "offs3": striped(idx3),
        "offs4": striped(idx4),
    }


def reference(xt_words, xt_scales, wt_words, wt_scales, ca, st, wb_words, wb_scales, so, offs, offs2, offs3, offs4):
    idx = unstriped(offs)
    idx2 = unstriped(offs2)
    idx3 = unstriped(offs3)
    idx4 = unstriped(offs4)
    xtu = unpack_weight(xt_words, xt_scales, "e4m3")
    wtu = unpack_weight(wt_words, wt_scales, "e2m1")
    wbu = unpack_weight(wb_words, wb_scales, "e5m2")
    wtidxg = wtu[:, idx]
    xtidx2g = xtu[:, idx2]
    a = wtidxg.T @ xtidx2g
    m1 = e4m3fn_values(ca)[:, idx3].reshape(R, J, I // J).max(axis=2)
    g1 = m1 * f64(st)
    hid = a * g1
    hidq = mxq(hid, 0, "e4m3")
    p = wbu.T @ hidq
    y = np.zeros((N, E))
    y[:, idx4] = p * f64(so)
    return y

from contextlib import ExitStack

import concourse.mybir as mybir
from concourse.masks import make_identity

K, T, J, R, V, D, I, N, E = 512, 1024, 256, 512, 1024, 2048, 1024, 256, 512
FLOPS = 2 * K * R * J + 2 * R * N * J

F32 = mybir.dt.float32
BF16 = mybir.dt.bfloat16
I32 = mybir.dt.int32
U32 = mybir.dt.uint32
U16 = mybir.dt.uint16
U8 = mybir.dt.uint8
FP8 = mybir.dt.float8_e4m3fn
E4M3X4 = mybir.dt.float8_e4m3fn_x4
E5M2X4 = mybir.dt.float8_e5m2_x4
E2M1X4 = mybir.dt.float4_e2m1fn_x4
MAX = mybir.AluOpType.max
MULT = mybir.AluOpType.mult
COPY = mybir.ActivationFunctionType.Copy

P = 128
PACK = 4
POOL = I // J
PARTS = ((0, 128), (128, 64), (192, 64))


def tile_list_pooledentries_kernel(
    tc, xt_words, xt_scales, wt_words, wt_scales, ca, st, wb_words, wb_scales, so, offs, offs2, offs3, offs4, out
):
    nc = tc.nc
    with ExitStack() as ctx:
        lists = ctx.enter_context(tc.tile_pool(name="lists", bufs=1))
        keep = ctx.enter_context(tc.tile_pool(name="keep", bufs=1))
        work = ctx.enter_context(tc.tile_pool(name="work", bufs=1))
        psum = ctx.enter_context(tc.psum_pool(name="psum", bufs=2))

        wt_list = lists.tile([P, R // 16], U16, name="wt_list")
        xt_list = lists.tile([P, J // 16], U16, name="xt_list")
        ca_list = lists.tile([P, I // 16], U16, name="ca_list")
        out_list = lists.tile([P, J // 16], U16, name="out_list")

        wt_w = keep.tile([P, V], U16, name="wt_w", align_bytes=64)
        wt_s = keep.tile([P, V], U8, name="wt_s", align_bytes=64)
        xt_w = keep.tile([P, T], U32, name="xt_w", align_bytes=64)
        xt_s = keep.tile([P, T], U8, name="xt_s", align_bytes=64)
        wb_w = keep.tile([P, N], U32, name="wb_w", align_bytes=64)
        wb_s = keep.tile([P, N], U8, name="wb_s", align_bytes=64)
        ca_rows = [keep.tile([P, D], U8, name=f"ca_rows{t}", align_bytes=64) for t in range(PACK)]
        st_cols = keep.tile([P, R // P], F32, name="st_cols")
        so_cols = keep.tile([P, N // P], F32, name="so_cols")
        ident = keep.tile([P, P], F32, name="ident")
        pages = [keep.tile([P, E], F32, name=f"page{b}", align_bytes=64) for b in range(N // P)]

        for plane in (wt_s, xt_s, wb_s):
            nc.vector.memset(plane[:].bitcast(I32), 0)
        make_identity(nc, ident[:])
        for page in pages:
            nc.gpsimd.memset(page[:], 0.0)

        def load_scales(plane, scales):
            for q in range(4):
                nc.sync.dma_start(plane[32 * q : 32 * q + 4, :].bitcast(I32), scales[0, 4 * q : 4 * q + 4, :].bitcast(I32))

        ca_dealt = ca.rearrange("(p t) d -> t p d", t=PACK)
        nc.sync.dma_start(wt_list[:], offs)
        nc.sync.dma_start(wt_w[:].bitcast(I32), wt_words[0].bitcast(I32))
        nc.sync.dma_start(ca_list[:], offs3)
        nc.sync.dma_start(ca_rows[0][:], ca_dealt[0])
        load_scales(wt_s, wt_scales)
        nc.sync.dma_start(xt_list[:], offs2)
        nc.sync.dma_start(xt_w[:].bitcast(I32), xt_words[0].rearrange("p c r -> p (c r)").bitcast(I32))
        load_scales(xt_s, xt_scales)
        for t in range(1, PACK):
            nc.sync.dma_start(ca_rows[t][:], ca_dealt[t])
        with nc.allow_non_contiguous_dma(reason="one value a partition"):
            nc.sync.dma_start(st_cols[:], st.rearrange("(q p) o -> p (q o)", p=P))
        nc.sync.dma_start(wb_w[:].bitcast(I32), wb_words[0].rearrange("p c r -> p (c r)").bitcast(I32))
        load_scales(wb_s, wb_scales)
        with nc.allow_non_contiguous_dma(reason="one value a partition"):
            nc.sync.dma_start(so_cols[:], so.rearrange("(b p) o -> p (b o)", p=P))
        nc.sync.dma_start(out_list[:], offs4)

        wt_wg = keep.tile([P, R], U16, name="wt_wg", align_bytes=64)
        wt_sg = keep.tile([P, R], U8, name="wt_sg", align_bytes=64)
        xt_wg = keep.tile([P, J], U32, name="xt_wg", align_bytes=64)
        xt_sg = keep.tile([P, J], U8, name="xt_sg", align_bytes=64)
        hid_w = keep.tile([P, J], U32, name="hid_w", align_bytes=64)
        hid_s = keep.tile([P, J], U8, name="hid_s", align_bytes=64)

        values = {}

        def look_up(part, t):
            j0, n = PARTS[part]
            picked = work.tile([P, POOL * n], U8, name=f"picked{t}", align_bytes=64)
            nc.vector.tensor_copy(picked[:], ca_rows[t][:].indirect(ca_list[:, POOL * j0 // 16 : POOL * (j0 + n) // 16]))
            if t % 2 == 0:
                values[part, t // 2] = work.tile([P, 2, POOL * n], F32, name=f"values{t // 2}", align_bytes=64)
            nc.scalar.copy(values[part, t // 2][:, t % 2, :], picked[:].bitcast(FP8))

        nc.vector.tensor_copy(wt_wg[:], wt_w[:].indirect(wt_list[:]))
        look_up(0, 0)
        nc.vector.tensor_copy(wt_sg[:], wt_s[:].indirect(wt_list[:]))
        nc.vector.tensor_copy(xt_wg[:], xt_w[:].indirect(xt_list[:]))
        nc.vector.tensor_copy(xt_sg[:], xt_s[:].indirect(xt_list[:]))

        scaled = keep.tile([P, R // P, J], F32, name="scaled", align_bytes=64)
        for b in range(2):
            sums = psum.tile([P, 2, J], F32, name="sums")
            for s in range(2):
                q = 2 * b + s
                nc.tensor.matmul_mx(
                    out=sums[:, s, :],
                    lhsT=wt_wg[:, q * P : (q + 1) * P].bitcast(E2M1X4),
                    lhsT_scale=wt_sg[:, q * P : (q + 1) * P],
                    rhs=xt_wg[:].bitcast(E4M3X4),
                    rhs_scale=xt_sg[:],
                    start=True,
                    stop=True,
                )
            for s in range(2):
                q = 2 * b + s
                nc.scalar.activation(scaled[:, q, :], sums[:, s, :], COPY, scale=st_cols[:, q : q + 1])
        a_st = []
        for h in range(J // P):
            turned = psum.tile([P, R], F32, name="turned")
            for q in range(R // P):
                nc.tensor.transpose(turned[:, q * P : (q + 1) * P], scaled[:, q, h * P : (h + 1) * P], ident[:])
            dealt = keep.tile([P, PACK, P], F32, name=f"dealt{h}", align_bytes=64)
            nc.scalar.copy(dealt[:], turned[:].rearrange("j (m t) -> j t m", t=PACK))
            back = psum.tile([P, PACK, P], F32, name="back")
            for t in range(PACK):
                nc.tensor.transpose(back[:, t, :], dealt[:, t, :], ident[:])
            a_st.append(back)

        def hidden(part):
            j0, n = PARTS[part]
            pairs = work.tile([P, 2, n, 2, 2], F32, name="pairs", align_bytes=64)
            for tp in range(2):
                v = values[part, tp][:].rearrange("p s (j u) -> p j s u", u=POOL)
                nc.vector.tensor_tensor(pairs[:, tp], v[:, :, :, 0:2], v[:, :, :, 2:4], MAX)
            top = work.tile([P, n, 2, 2], F32, name="top", align_bytes=64)
            w = pairs[:].rearrange("p tp j s u -> p j tp s u")
            nc.vector.tensor_tensor(top[:], w[:, :, :, :, 0], w[:, :, :, :, 1], MAX)
            hid = work.tile([P, n, PACK], BF16, name="hid", align_bytes=64)
            h, jh = divmod(j0, P)
            nc.vector.tensor_tensor(
                hid[:], top[:].rearrange("p j tp s -> p j (tp s)"), a_st[h][:, :, jh : jh + n].rearrange("p t j -> p j t"), MULT
            )
            nc.vector.quantize_mx(
                out=hid_w[:, j0 : j0 + n].bitcast(E4M3X4),
                scales=hid_s[:, j0 : j0 + n],
                in_=hid[:].rearrange("p j t -> p (j t)"),
            )

        def put(part):
            j0, n = PARTS[part]
            c0 = j0 + n - P
            prod = psum.tile([P, 2, J], F32, name="sums")
            for b in range(N // P):
                nc.tensor.matmul_mx(
                    out=prod[:, b, 0:P],
                    lhsT=wb_w[:, b * P : (b + 1) * P].bitcast(E5M2X4),
                    lhsT_scale=wb_s[:, b * P : (b + 1) * P],
                    rhs=hid_w[:, c0 : c0 + P].bitcast(E4M3X4),
                    rhs_scale=hid_s[:, c0 : c0 + P],
                    start=True,
                    stop=True,
                )
            rows = keep.tile([P, N // P, n], F32, name=f"rows{part}", align_bytes=64)
            nc.scalar.copy(rows[:], prod[:, :, P - n : P])
            for b in range(N // P):
                nc.scalar.activation(
                    pages[b][:].indirect(out_list[:, j0 // 16 : (j0 + n) // 16]), rows[:, b, :], COPY, scale=so_cols[:, b : b + 1]
                )

        for t in range(1, PACK):
            look_up(0, t)
        for part in range(len(PARTS)):
            if part + 1 < len(PARTS):
                for t in range(PACK):
                    look_up(part + 1, t)
            hidden(part)
            put(part)

        nc.sync.dma_start(out[0:P, :], pages[0][:])
        nc.scalar.dma_start(out[P : 2 * P, :], pages[1][:])
